import numpy as np
import ml_dtypes


def mxq(x, axis, fmt="e4m3"):
    dtype, down = {"e4m3": (ml_dtypes.float8_e4m3fn, 7), "e5m2": (ml_dtypes.float8_e5m2, 14)}[fmt]
    v = np.moveaxis(np.asarray(x, np.float32).astype(ml_dtypes.bfloat16).astype(np.float64), axis, -1)
    blocks = v.reshape(v.shape[:-1] + (-1, 32))
    amax = np.abs(blocks).max(-1, keepdims=True)
    byte = np.maximum(np.where(amax > 0, np.frexp(amax)[1] - 1 + 127, 0) - down, 1)
    scale = np.exp2(byte - 127.0)
    codes = (blocks / scale).astype(np.float32).astype(dtype).astype(np.float64)
    return np.moveaxis((codes * scale).reshape(v.shape), -1, axis)


WIDE = False


def mx_kscale(k):
    if not WIDE:
        return np.ones(k)
    levels = np.array([10, -10, 5, -5, 0])
    if k % 512:
        return np.exp2(np.random.permutation(np.resize(levels, k // 32))).repeat(32)
    a = np.empty((k // 512, 16))
    for p in range(k // 512):
        a[p, :8] = np.random.permutation(np.resize(levels, 8))
        for g in range(8):
            far = levels[np.abs(levels - a[p, g]) >= 10]
            a[p, g + 8] = far[np.random.randint(len(far))]
    return np.exp2(a.ravel()).repeat(32)


def f64(x):
    return np.asarray(x).astype(np.float64)


def striped(idx):
    return np.tile(idx.reshape(-1, 16).T, (8, 1)).astype(np.uint16)


def unstriped(offs):
    return offs[:16].T.reshape(-1).astype(np.int64)


def striped8(idx):
    return np.concatenate([x.reshape(-1, 16).T for x in idx]).astype(np.uint16)


def runs(offs, k):
    lists = np.stack([offs[16 * r : 16 * r + 16].T.reshape(-1) for r in range(8)]).astype(np.int64)
    return lists[np.arange(k) % 512 // 64]


def pack_weight(w):
    k, n = w.shape
    w = f64(np.asarray(w, np.float32).astype(ml_dtypes.bfloat16)).reshape(k // 32, 32, n)
    amax = np.abs(w).max(1)
    byte = np.clip(np.where(amax > 0, np.frexp(amax)[1] - 1 + 127 - 7, 1), 1, 254)
    scaled = (w * np.exp2(127.0 - byte)[:, None, :]).reshape(k, n).astype(np.float32)
    words = np.ascontiguousarray(scaled.reshape(k // 512, 128, 4, n).transpose(0, 1, 3, 2)).astype(ml_dtypes.float8_e4m3fn).view(np.uint8)
    return words, np.ascontiguousarray(byte.astype(np.uint8).reshape(k // 512, 16, n))


def unpack_weight(words, scales):
    g, p, n, _ = words.shape
    vals = np.ascontiguousarray(words).view(ml_dtypes.float8_e4m3fn).astype(np.float64) * np.repeat(np.exp2(scales.astype(np.float64) - 127.0), 8, axis=1)[..., None]
    return vals.transpose(0, 1, 3, 2).reshape(g * 512, n)


K, T, S, V, N, H, U = 512, 2048, 1024, 512, 512, 512, 1024


def setup_inputs():
    n = np.random.standard_normal
    s = mx_kscale(K)[:, None]
    u = mx_kscale(H)
    packed_xT = pack_weight(n((K, T)) * s)
    return {
        "x_words": packed_xT[0],
        "x_scales": packed_xT[1],
        "w1": (n((K, H)) / np.sqrt(K) / s).astype(np.float32),
        "gn": (np.random.uniform(0.5, 1.5, (H, 1)) * u[:, None]).astype(np.float32),
        "w2": (n((H, N)) / np.sqrt(H) / u[:, None]).astype(np.float32),
        "mem": n((N, U)).astype(np.float32),
        "offs": striped(np.random.permutation(T)[:S]),
        "n1": striped8(np.stack([np.random.permutation(S) for _ in range(8)])),
        "n2": striped8(np.stack([np.random.permutation(U)[:V] for _ in range(8)])),
        "n3": striped8(np.stack([np.random.permutation(U) for _ in range(8)])),
    }


def reference(x_words, x_scales, w1, gn, w2, mem, offs, n1, n2, n3):
    xq = unpack_weight(x_words, x_scales)[:, unstriped(offs)]
    y = mxq(f64(w1), 0, "e4m3").T @ xq
    ln = y[np.arange(H)[:, None], runs(n1, H)]
    mx = ln.reshape(H, V, 2).max(axis=2)
    mn = ln.reshape(H, V, 2).min(axis=2)
    z = f64(gn) * (mx - (0.5 * mn))
    h = mxq(f64(w2), 0, "e4m3").T @ mxq(z, 0, "e4m3")
    pg = f64(mem).copy()
    pg[np.arange(N)[:, None], runs(n2, N)] = h
    return pg - (0.5 * (pg[np.arange(N)[:, None], runs(n3, N)]))

@@ -1,0 +1,232 @@
+from contextlib import ExitStack
+
+import concourse.mybir as mybir
+
+K, T, S, V, N, H, U = 512, 2048, 1024, 512, 512, 512, 1024
+FLOPS = 2 * K * H * S + 2 * H * N * V
+
+F32 = mybir.dt.float32
+BF16 = mybir.dt.bfloat16
+I32 = mybir.dt.int32
+U32 = mybir.dt.uint32
+U16 = mybir.dt.uint16
+U8 = mybir.dt.uint8
+FP8X4 = mybir.dt.float8_e4m3fn_x4
+ALU = mybir.AluOpType
+COPY = mybir.ActivationFunctionType.Copy
+
+P = 128
+PACK = 4
+BANK = 512
+LANE = 16
+HV = V // 2
+
+
+def tile_picked_laypgappagem_none_p_kernel(
+    tc, x_words, x_scales, w1, gn, w2, mem, offs, n1, n2, n3, out
+):
+    nc = tc.nc
+    with ExitStack() as ctx:
+        lists = ctx.enter_context(tc.tile_pool(name="lists", bufs=1))
+        keep = ctx.enter_context(tc.tile_pool(name="keep", bufs=1))
+        psum = ctx.enter_context(tc.psum_pool(name="psum", bufs=1))
+
+        offs_sb = lists.tile([P, S // LANE], U16, name="offs_sb")
+        n1_sb = lists.tile([P, S // LANE], U16, name="n1_sb")
+        n2_sb = lists.tile([P, V // LANE], U16, name="n2_sb")
+        n3_sb = lists.tile([P, U // LANE], U16, name="n3_sb")
+
+        def entries(list_sb, first, count):
+            return list_sb[:, first // LANE : (first + count) // LANE]
+
+        scale_table = keep.tile([P, T], U8, name="scale_table", align_bytes=64)
+        nc.gpsimd.memset(scale_table[:].bitcast(I32), 0)
+        scale_rows = keep.tile([P, T], U8, name="scale_rows", align_bytes=64)
+        nc.sync.dma_start(offs_sb[:], offs)
+        gain = keep.tile([P, PACK], F32, name="gain")
+        nc.scalar.dma_start(out=gain[:], in_=gn.rearrange("(p t) o -> p (t o)", t=PACK))
+        for q in range(4):
+            nc.sync.dma_start(
+                out=scale_rows[32 * q : 32 * q + 4, :].bitcast(I32),
+                in_=x_scales[0, 4 * q : 4 * q + 4, :].bitcast(I32),
+            )
+        w1_rows = w1.rearrange("(p j) c -> p j c", j=PACK)
+        w1_raw = []
+        for half in range(2):
+            raw = keep.tile([P, PACK, H // 2], F32, name=f"w1_raw{half}")
+            nc.sync.dma_start(out=raw[:], in_=w1_rows[:, :, half * (H // 2) : (half + 1) * (H // 2)])
+            w1_raw.append(raw)
+        word_table = keep.tile([P, T], U32, name="word_table", align_bytes=64)
+        nc.sync.dma_start(
+            out=word_table[:].bitcast(I32),
+            in_=x_words[0].rearrange("p n r -> p (n r)").bitcast(I32),
+        )
+        nc.sync.dma_start(n1_sb[:], n1)
+        w2_raw = keep.tile([P, PACK, N], F32, name="w2_raw")
+        nc.sync.dma_start(out=w2_raw[:], in_=w2.rearrange("(p j) c -> p j c", j=PACK))
+        nc.sync.dma_start(n2_sb[:], n2)
+        mem_rows = mem.rearrange("(p t) w -> t p w", t=PACK)
+        out_rows = out.rearrange("(p t) w -> t p w", t=PACK)
+        page = []
+        for t in range(PACK):
+            pg = keep.tile([P, U], F32, name=f"page{t}")
+            nc.sync.dma_start(out=pg[:], in_=mem_rows[t])
+            page.append(pg)
+        nc.sync.dma_start(n3_sb[:], n3)
+
+        def dealt(grouped):
+            return grouped[:].rearrange("p (t m j) -> p m j t", t=PACK, j=PACK)
+
+        def quantise(name, values, width):
+            codes = keep.tile([P, width], U32, name=name + "_codes", align_bytes=64)
+            scales = keep.tile([P, width], U8, name=name + "_scales", align_bytes=64)
+            nc.vector.quantize_mx(out=codes[:].bitcast(FP8X4), scales=scales[:], in_=values)
+            return codes, scales
+
+        half_gain = keep.tile([P, PACK], F32, name="half_gain")
+        positive = keep.tile([P, PACK], F32, name="positive")
+        slope = keep.tile([P, PACK], F32, name="slope")
+        factor = keep.tile([P, PACK], F32, name="factor")
+        nc.vector.tensor_scalar_mul(half_gain[:], gain[:], 0.5)
+        nc.vector.tensor_single_scalar(positive[:], gain[:], 0.0, ALU.is_ge)
+        nc.vector.tensor_scalar(slope[:], positive[:], 1.5, -2.0, ALU.mult, ALU.add)
+        nc.vector.tensor_scalar(factor[:], positive[:], 3.0, -1.0, ALU.mult, ALU.add)
+
+        for q in range(4):
+            rows = slice(32 * q, 32 * q + 4)
+            nc.vector.tensor_copy(scale_table[rows, :].bitcast(I32), scale_rows[rows, :].bitcast(I32))
+        x_scale = keep.tile([P, S], U8, name="x_scale", align_bytes=64)
+        nc.vector.tensor_copy(x_scale[:], scale_table[:].indirect(offs_sb[:]))
+
+
+        w1_bf = keep.tile([P, PACK * H], BF16, name="w1_bf", align_bytes=64)
+        for half in range(2):
+            nc.scalar.copy(
+                out=dealt(w1_bf)[:, half * 64 : (half + 1) * 64],
+                in_=w1_raw[half][:].rearrange("p j (m t) -> p m j t", t=PACK),
+            )
+        w1_codes, w1_scales = quantise("w1", w1_bf[:], H)
+
+
+        x_code = []
+        for half in range(2):
+            xc = keep.tile([P, BANK], U32, name=f"x_code{half}", align_bytes=64)
+            nc.vector.tensor_copy(xc[:], word_table[:].indirect(entries(offs_sb, half * BANK, BANK)))
+            x_code.append(xc)
+
+        y_bank = {}
+        for t, half in ((0, 0), (1, 0), (0, 1), (1, 1), (2, 0), (2, 1), (3, 0), (3, 1)):
+            if True:
+                bank = psum.tile([P, BANK], F32, name=f"y{t}_{half}", tag=f"bank{PACK * half + t}")
+                cols = slice(P * t, P * (t + 1))
+                nc.tensor.matmul_mx(
+                    out=bank[:],
+                    lhsT=w1_codes[:, cols].bitcast(FP8X4),
+                    lhsT_scale=w1_scales[:, cols],
+                    rhs=x_code[half][:].bitcast(FP8X4),
+                    rhs_scale=x_scale[:, half * BANK : (half + 1) * BANK],
+                    start=True,
+                    stop=True,
+                )
+                y_bank[t, half] = bank
+
+
+        y = [keep.tile([P, S], F32, name=f"y_sb{t}") for t in range(PACK)]
+
+        def leave_y(t, half, on_vector):
+            dst = y[t][:, half * BANK : (half + 1) * BANK]
+            if on_vector:
+                nc.vector.tensor_scalar_mul(dst, y_bank[t, half][:], half_gain[:, t : t + 1])
+            else:
+                nc.scalar.activation(dst, y_bank[t, half][:], COPY, scale=half_gain[:, t : t + 1])
+
+        lined = {}
+
+        def line_up(t, half):
+            ln = keep.tile([P, 2 * HV], F32, name=f"lined{t}_{half}")
+            nc.scalar.activation(ln[:], y[t][:].indirect(entries(n1_sb, half * 2 * HV, 2 * HV)), COPY)
+            lined[t, half] = ln
+
+        z_planes = [keep.tile([P, PACK, HV], BF16, name=f"z_planes{half}") for half in range(2)]
+
+        def make_z(t):
+            diff = [keep.tile([P, HV], F32, name=f"diff{t}_{half}") for half in range(2)]
+            bent = [keep.tile([P, HV], F32, name=f"bent{t}_{half}") for half in range(2)]
+            for half in range(2):
+                ln = lined[t, half]
+                nc.vector.tensor_tensor(diff[half][:], ln[:, 1::2], ln[:, 0::2], ALU.subtract)
+            for half in range(2):
+                nc.vector.scalar_tensor_tensor(
+                    bent[half][:], diff[half][:], slope[:, t : t + 1], diff[half][:], ALU.mult, ALU.max
+                )
+            for half in range(2):
+                nc.vector.scalar_tensor_tensor(
+                    z_planes[half][:, t, :], bent[half][:], factor[:, t : t + 1], lined[t, half][:, 0::2], ALU.mult, ALU.add
+                )
+
+        h = [keep.tile([P, V], F32, name=f"h_sb{t}") for t in range(PACK)]
+
+        def second_product(half):
+            z_bf = keep.tile([P, HV, PACK], BF16, name=f"z_bf{half}", align_bytes=64)
+            if half == 0:
+                nc.vector.tensor_copy(out=z_bf[:], in_=z_planes[half][:].rearrange("p t v -> p v t"))
+            else:
+                nc.scalar.copy(out=z_bf[:], in_=z_planes[half][:].rearrange("p t v -> p v t"))
+            z_codes, z_scales = quantise(f"z{half}", z_bf[:].rearrange("p v t -> p (v t)"), HV)
+            for t in range(PACK):
+                bank = psum.tile([P, HV], F32, name=f"h{t}_{half}", tag=f"bank{PACK * half + t}")
+                cols = slice(P * t, P * (t + 1))
+                nc.tensor.matmul_mx(
+                    out=bank[:],
+                    lhsT=w2_codes[:, cols].bitcast(FP8X4),
+                    lhsT_scale=w2_scales[:, cols],
+                    rhs=z_codes[:].bitcast(FP8X4),
+                    rhs_scale=z_scales[:],
+                    start=True,
+                    stop=True,
+                )
+                nc.scalar.copy(out=h[t][:, half * HV : (half + 1) * HV], in_=bank[:])
+
+        def put(t, first, count):
+            nc.vector.tensor_copy(page[t][:].indirect(entries(n2_sb, first, count)), h[t][:, first : first + count])
+
+        def finish(t, first, count, on_vector):
+            cols = slice(first, first + count)
+            fetched = keep.tile([P, count], F32, name=f"fetched{t}_{first}")
+            result = keep.tile([P, count], F32, name=f"result{t}_{first}")
+            window = page[t][:].indirect(entries(n3_sb, first, count))
+            if on_vector:
+                nc.vector.tensor_scalar(fetched[:], window, -0.5, 0.0, ALU.mult, ALU.add)
+                nc.vector.tensor_tensor(result[:], fetched[:], page[t][:, cols], ALU.add)
+            else:
+                nc.scalar.activation(fetched[:], window, COPY, scale=-0.5)
+                nc.gpsimd.tensor_tensor(result[:], fetched[:], page[t][:, cols], ALU.add)
+            nc.sync.dma_start(out=out_rows[t][:, cols], in_=result[:])
+
+        leave_y(0, 0, False)
+        leave_y(1, 0, False)
+        leave_y(0, 1, False)
+        leave_y(1, 1, True)
+        for t in (2, 3):
+            leave_y(t, 0, True)
+            leave_y(t, 1, True)
+        w2_bf = keep.tile([P, PACK * N], BF16, name="w2_bf", align_bytes=64)
+        nc.vector.tensor_copy(out=dealt(w2_bf), in_=w2_raw[:].rearrange("p j (m t) -> p m j t", t=PACK))
+        w2_codes, w2_scales = quantise("w2", w2_bf[:], N)
+        for t in range(PACK):
+            line_up(t, 0)
+            line_up(t, 1)
+            make_z(t)
+        second_product(0)
+        second_product(1)
+        put(0, 0, HV)
+        put(0, HV, HV)
+        finish(0, 0, BANK, False)
+        finish(0, BANK, BANK, False)
+        for t in (1, 2):
+            put(t, 0, V)
+            finish(t, 0, BANK, False)
+            finish(t, BANK, BANK, False)
+        put(3, 0, V)
+        for quarter in range(4):
+            finish(3, quarter * 256, 256, quarter >= 2)

@@ -62,8 +62,12 @@ def tile_picked_laypgappagem_none_p_kernel(
             in_=x_words[0].rearrange("p n r -> p (n r)").bitcast(I32),
         )
         nc.sync.dma_start(n1_sb[:], n1)
-        w2_raw = keep.tile([P, PACK, N], F32, name="w2_raw")
-        nc.sync.dma_start(out=w2_raw[:], in_=w2.rearrange("(p j) c -> p j c", j=PACK))
+        w2_rows = w2.rearrange("(p j) c -> p j c", j=PACK)
+        w2_raw = []
+        for half in range(2):
+            raw = keep.tile([P, PACK, N // 2], F32, name=f"w2_raw{half}")
+            nc.sync.dma_start(out=raw[:], in_=w2_rows[:, :, half * (N // 2) : (half + 1) * (N // 2)])
+            w2_raw.append(raw)
         nc.sync.dma_start(n2_sb[:], n2)
         mem_rows = mem.rearrange("(p t) w -> t p w", t=PACK)
         out_rows = out.rearrange("(p t) w -> t p w", t=PACK)
@@ -143,36 +147,32 @@ def tile_picked_laypgappagem_none_p_kernel(
         lined = {}
 
         def line_up(t, half):
-            ln = keep.tile([P, 2 * HV], F32, name=f"lined{t}_{half}")
+            ln = keep.tile([P, 2 * HV], F32, name=f"lined{t}_{half}", tag=f"lined{t}")
             nc.scalar.activation(ln[:], y[t][:].indirect(entries(n1_sb, half * 2 * HV, 2 * HV)), COPY)
             lined[t, half] = ln
 
-        z_planes = [keep.tile([P, PACK, HV], BF16, name=f"z_planes{half}") for half in range(2)]
+        z_planes = [keep.tile([P, PACK, HV], BF16, name=f"z_planes{half}", tag=f"z_planes{half}") for half in range(2)]
 
-        def make_z(t):
-            diff = [keep.tile([P, HV], F32, name=f"diff{t}_{half}") for half in range(2)]
-            bent = [keep.tile([P, HV], F32, name=f"bent{t}_{half}") for half in range(2)]
-            for half in range(2):
+        def make_z(ts, half):
+            diff = {t: keep.tile([P, HV], F32, name=f"diff{t}_{half}") for t in ts}
+            bent = {t: keep.tile([P, HV], F32, name=f"bent{t}_{half}") for t in ts}
+            for t in ts:
                 ln = lined[t, half]
-                nc.vector.tensor_tensor(diff[half][:], ln[:, 1::2], ln[:, 0::2], ALU.subtract)
-            for half in range(2):
+                nc.vector.tensor_tensor(diff[t][:], ln[:, 1::2], ln[:, 0::2], ALU.subtract)
+            for t in ts:
                 nc.vector.scalar_tensor_tensor(
-                    bent[half][:], diff[half][:], slope[:, t : t + 1], diff[half][:], ALU.mult, ALU.max
+                    bent[t][:], diff[t][:], slope[:, t : t + 1], diff[t][:], ALU.mult, ALU.max
                 )
-            for half in range(2):
+            for t in ts:
                 nc.vector.scalar_tensor_tensor(
-                    z_planes[half][:, t, :], bent[half][:], factor[:, t : t + 1], lined[t, half][:, 0::2], ALU.mult, ALU.add
+                    z_planes[half][:, t, :], bent[t][:], factor[:, t : t + 1], lined[t, half][:, 0::2], ALU.mult, ALU.add
                 )
 
-        h = [keep.tile([P, V], F32, name=f"h_sb{t}") for t in range(PACK)]
+        z_bf = [keep.tile([P, HV, PACK], BF16, name=f"z_bf{half}", align_bytes=64) for half in range(2)]
+        h_bank = {}
 
         def second_product(half):
-            z_bf = keep.tile([P, HV, PACK], BF16, name=f"z_bf{half}", align_bytes=64)
-            if half == 0:
-                nc.vector.tensor_copy(out=z_bf[:], in_=z_planes[half][:].rearrange("p t v -> p v t"))
-            else:
-                nc.scalar.copy(out=z_bf[:], in_=z_planes[half][:].rearrange("p t v -> p v t"))
-            z_codes, z_scales = quantise(f"z{half}", z_bf[:].rearrange("p v t -> p (v t)"), HV)
+            z_codes, z_scales = quantise(f"z{half}", z_bf[half][:].rearrange("p v t -> p (v t)"), HV)
             for t in range(PACK):
                 bank = psum.tile([P, HV], F32, name=f"h{t}_{half}", tag=f"bank{PACK * half + t}")
                 cols = slice(P * t, P * (t + 1))
@@ -185,48 +185,66 @@ def tile_picked_laypgappagem_none_p_kernel(
                     start=True,
                     stop=True,
                 )
-                nc.scalar.copy(out=h[t][:, half * HV : (half + 1) * HV], in_=bank[:])
+                h_bank[t, half] = bank
 
-        def put(t, first, count):
-            nc.vector.tensor_copy(page[t][:].indirect(entries(n2_sb, first, count)), h[t][:, first : first + count])
+        def leave_h(dst, t, half):
+            nc.scalar.copy(out=dst, in_=h_bank[t, half][:])
 
-        def finish(t, first, count, on_vector):
+        def put(t, first, count, values):
+            nc.vector.tensor_copy(page[t][:].indirect(entries(n2_sb, first, count)), values)
+
+        def finish(t, first, count):
             cols = slice(first, first + count)
             fetched = keep.tile([P, count], F32, name=f"fetched{t}_{first}")
             result = keep.tile([P, count], F32, name=f"result{t}_{first}")
             window = page[t][:].indirect(entries(n3_sb, first, count))
-            if on_vector:
-                nc.vector.tensor_scalar(fetched[:], window, -0.5, 0.0, ALU.mult, ALU.add)
-                nc.vector.tensor_tensor(result[:], fetched[:], page[t][:, cols], ALU.add)
-            else:
-                nc.scalar.activation(fetched[:], window, COPY, scale=-0.5)
-                nc.gpsimd.tensor_tensor(result[:], fetched[:], page[t][:, cols], ALU.add)
+            nc.scalar.activation(fetched[:], window, COPY, scale=-0.5)
+            nc.vector.tensor_tensor(result[:], fetched[:], page[t][:, cols], ALU.add)
             nc.sync.dma_start(out=out_rows[t][:, cols], in_=result[:])
 
-        leave_y(0, 0, False)
-        leave_y(1, 0, False)
-        leave_y(0, 1, False)
-        leave_y(1, 1, True)
-        for t in (2, 3):
-            leave_y(t, 0, True)
-            leave_y(t, 1, True)
         w2_bf = keep.tile([P, PACK * N], BF16, name="w2_bf", align_bytes=64)
-        nc.vector.tensor_copy(out=dealt(w2_bf), in_=w2_raw[:].rearrange("p j (m t) -> p m j t", t=PACK))
+        nc.scalar.copy(out=dealt(w2_bf)[:, 0:64], in_=w2_raw[0][:].rearrange("p j (m t) -> p m j t", t=PACK))
+        for t, half in ((0, 0), (1, 0), (0, 1), (1, 1), (2, 0), (2, 1), (3, 0), (3, 1)):
+            leave_y(t, half, t >= 2)
+        nc.vector.tensor_copy(out=dealt(w2_bf)[:, 64:128], in_=w2_raw[1][:].rearrange("p j (m t) -> p m j t", t=PACK))
         w2_codes, w2_scales = quantise("w2", w2_bf[:], N)
         for t in range(PACK):
             line_up(t, 0)
-            line_up(t, 1)
-            make_z(t)
+        make_z((0, 1), 0)
+        make_z((2, 3), 0)
+        line_up(0, 1)
+        line_up(1, 1)
+        nc.vector.tensor_copy(out=z_bf[0][:], in_=z_planes[0][:].rearrange("p t v -> p v t"))
         second_product(0)
+        line_up(2, 1)
+        line_up(3, 1)
+        make_z((0, 1), 1)
+        make_z((2, 3), 1)
+        h0 = keep.tile([P, V], F32, name="h0", tag="h_first_last")
+        h2 = keep.tile([P, V], F32, name="h2")
+        leave_h(h0[:, :HV], 0, 0)
+        leave_h(h2[:, :HV], 2, 0)
+        nc.scalar.copy(out=z_bf[1][:], in_=z_planes[1][:].rearrange("p t v -> p v t"))
+        h1_low = keep.tile([P, HV], F32, name="h1_low", tag="z_planes1")
+        h1_high = keep.tile([P, HV], F32, name="h1_high")
+        leave_h(h1_low[:], 1, 0)
         second_product(1)
-        put(0, 0, HV)
-        put(0, HV, HV)
-        finish(0, 0, BANK, False)
-        finish(0, BANK, BANK, False)
+        leave_h(h0[:, HV:], 0, 1)
+        leave_h(h1_high[:], 1, 1)
+        leave_h(h2[:, HV:], 2, 1)
+        put(0, 0, HV, h0[:, :HV])
+        put(0, HV, HV, h0[:, HV:])
+        put(1, 0, HV, h1_low[:])
+        put(1, HV, HV, h1_high[:])
+        put(2, 0, V, h2[:])
+        finish(0, 0, BANK)
+        finish(0, BANK, BANK)
+        h3 = keep.tile([P, V], F32, name="h3", tag="h_first_last")
+        leave_h(h3[:, :HV], 3, 0)
+        leave_h(h3[:, HV:], 3, 1)
+        put(3, 0, V, h3[:])
         for t in (1, 2):
-            put(t, 0, V)
-            finish(t, 0, BANK, False)
-            finish(t, BANK, BANK, False)
-        put(3, 0, V)
+            finish(t, 0, BANK)
+            finish(t, BANK, BANK)
         for quarter in range(4):
-            finish(3, quarter * 256, 256, quarter >= 2)
+            finish(3, quarter * 256, 256)

@@ -154,7 +154,7 @@ def tile_picked_laypgappagem_none_p_kernel(
         z_planes = [keep.tile([P, PACK, HV], BF16, name=f"z_planes{half}", tag=f"z_planes{half}") for half in range(2)]
 
         def make_z(ts, half):
-            diff = {t: keep.tile([P, HV], F32, name=f"diff{t}_{half}") for t in ts}
+            diff = {t: keep.tile([P, HV], F32, name=f"diff{t}_{half}", tag="z_planes0" if (t, half) == (1, 1) else f"diff{t}_{half}") for t in ts}
             bent = {t: keep.tile([P, HV], F32, name=f"bent{t}_{half}") for t in ts}
             for t in ts:
                 ln = lined[t, half]
@@ -193,19 +193,22 @@ def tile_picked_laypgappagem_none_p_kernel(
         def put(t, first, count, values):
             nc.vector.tensor_copy(page[t][:].indirect(entries(n2_sb, first, count)), values)
 
-        def finish(t, first, count):
+        def finish(t, first, count, fetch_on_vector, add_engine):
             cols = slice(first, first + count)
             fetched = keep.tile([P, count], F32, name=f"fetched{t}_{first}")
             result = keep.tile([P, count], F32, name=f"result{t}_{first}")
             window = page[t][:].indirect(entries(n3_sb, first, count))
-            nc.scalar.activation(fetched[:], window, COPY, scale=-0.5)
-            nc.vector.tensor_tensor(result[:], fetched[:], page[t][:, cols], ALU.add)
+            if fetch_on_vector:
+                nc.vector.tensor_scalar(fetched[:], window, -0.5, 0.0, ALU.mult, ALU.add)
+            else:
+                nc.scalar.activation(fetched[:], window, COPY, scale=-0.5)
+            add_engine.tensor_tensor(result[:], fetched[:], page[t][:, cols], ALU.add)
             nc.sync.dma_start(out=out_rows[t][:, cols], in_=result[:])
 
         w2_bf = keep.tile([P, PACK * N], BF16, name="w2_bf", align_bytes=64)
         nc.scalar.copy(out=dealt(w2_bf)[:, 0:64], in_=w2_raw[0][:].rearrange("p j (m t) -> p m j t", t=PACK))
         for t, half in ((0, 0), (1, 0), (0, 1), (1, 1), (2, 0), (2, 1), (3, 0), (3, 1)):
-            leave_y(t, half, t >= 2)
+            leave_y(t, half, t >= 2 or (t, half) == (0, 1))
         nc.vector.tensor_copy(out=dealt(w2_bf)[:, 64:128], in_=w2_raw[1][:].rearrange("p j (m t) -> p m j t", t=PACK))
         w2_codes, w2_scales = quantise("w2", w2_bf[:], N)
         for t in range(PACK):
@@ -220,31 +223,30 @@ def tile_picked_laypgappagem_none_p_kernel(
         line_up(3, 1)
         make_z((0, 1), 1)
         make_z((2, 3), 1)
-        h0 = keep.tile([P, V], F32, name="h0", tag="h_first_last")
-        h2 = keep.tile([P, V], F32, name="h2")
-        leave_h(h0[:, :HV], 0, 0)
-        leave_h(h2[:, :HV], 2, 0)
+        h = {t: keep.tile([P, V], F32, name=f"h{t}") for t in (2, 3)}
+        for t in (2, 3):
+            leave_h(h[t][:, :HV], t, 0)
+        h0_low = keep.tile([P, HV], F32, name="h0_low", tag="diff3_1")
+        h0_high = keep.tile([P, HV], F32, name="h0_high")
+        leave_h(h0_low[:], 0, 0)
         nc.scalar.copy(out=z_bf[1][:], in_=z_planes[1][:].rearrange("p t v -> p v t"))
         h1_low = keep.tile([P, HV], F32, name="h1_low", tag="z_planes1")
         h1_high = keep.tile([P, HV], F32, name="h1_high")
         leave_h(h1_low[:], 1, 0)
         second_product(1)
-        leave_h(h0[:, HV:], 0, 1)
+        leave_h(h0_high[:], 0, 1)
         leave_h(h1_high[:], 1, 1)
-        leave_h(h2[:, HV:], 2, 1)
-        put(0, 0, HV, h0[:, :HV])
-        put(0, HV, HV, h0[:, HV:])
+        leave_h(h[2][:, HV:], 2, 1)
+        leave_h(h[3][:, HV:], 3, 1)
+        put(0, 0, HV, h0_low[:])
+        put(0, HV, HV, h0_high[:])
         put(1, 0, HV, h1_low[:])
         put(1, HV, HV, h1_high[:])
-        put(2, 0, V, h2[:])
-        finish(0, 0, BANK)
-        finish(0, BANK, BANK)
-        h3 = keep.tile([P, V], F32, name="h3", tag="h_first_last")
-        leave_h(h3[:, :HV], 3, 0)
-        leave_h(h3[:, HV:], 3, 1)
-        put(3, 0, V, h3[:])
-        for t in (1, 2):
-            finish(t, 0, BANK)
-            finish(t, BANK, BANK)
-        for quarter in range(4):
-            finish(3, quarter * 256, 256)
+        for t in range(PACK - 1):
+            finish(t, 0, BANK, False, nc.gpsimd)
+            finish(t, BANK, BANK, False, nc.gpsimd)
+            if t < 2:
+                put(t + 2, 0, V, h[t + 2][:])
+        finish(3, 0, 320, False, nc.vector)
+        finish(3, 640, 384, True, nc.vector)
+        finish(3, 320, 320, False, nc.vector)

@@ -43,13 +43,13 @@ def tile_picked_laypgappagem_none_p_kernel(
         nc.gpsimd.memset(scale_table[:].bitcast(I32), 0)
         scale_rows = keep.tile([P, T], U8, name="scale_rows", align_bytes=64)
         nc.sync.dma_start(offs_sb[:], offs)
-        gain = keep.tile([P, PACK], F32, name="gain")
-        nc.scalar.dma_start(out=gain[:], in_=gn.rearrange("(p t) o -> p (t o)", t=PACK))
         for q in range(4):
             nc.sync.dma_start(
                 out=scale_rows[32 * q : 32 * q + 4, :].bitcast(I32),
                 in_=x_scales[0, 4 * q : 4 * q + 4, :].bitcast(I32),
             )
+        gain = keep.tile([P, PACK], F32, name="gain")
+        nc.sync.dma_start(out=gain[:], in_=gn.rearrange("(p t) o -> p (t o)", t=PACK))
         w1_rows = w1.rearrange("(p j) c -> p j c", j=PACK)
         w1_raw = []
         for half in range(2):
@@ -91,10 +91,10 @@ def tile_picked_laypgappagem_none_p_kernel(
         positive = keep.tile([P, PACK], F32, name="positive")
         slope = keep.tile([P, PACK], F32, name="slope")
         factor = keep.tile([P, PACK], F32, name="factor")
-        nc.vector.tensor_scalar_mul(half_gain[:], gain[:], 0.5)
-        nc.vector.tensor_single_scalar(positive[:], gain[:], 0.0, ALU.is_ge)
-        nc.vector.tensor_scalar(slope[:], positive[:], 1.5, -2.0, ALU.mult, ALU.add)
-        nc.vector.tensor_scalar(factor[:], positive[:], 3.0, -1.0, ALU.mult, ALU.add)
+        nc.gpsimd.tensor_scalar(half_gain[:], gain[:], 0.5, 0.0, ALU.mult, ALU.add)
+        nc.gpsimd.tensor_scalar(positive[:], gain[:], 0.0, 1.0, ALU.is_ge, ALU.mult)
+        nc.gpsimd.tensor_scalar(slope[:], positive[:], 1.5, -2.0, ALU.mult, ALU.add)
+        nc.gpsimd.tensor_scalar(factor[:], positive[:], 3.0, -1.0, ALU.mult, ALU.add)
 
         for q in range(4):
             rows = slice(32 * q, 32 * q + 4)

from contextlib import ExitStack

import concourse.mybir as mybir

K, T, S, V, N, H, U = 512, 2048, 1024, 512, 512, 512, 1024
FLOPS = 2 * K * H * S + 2 * H * N * V

F32 = mybir.dt.float32
BF16 = mybir.dt.bfloat16
I32 = mybir.dt.int32
U32 = mybir.dt.uint32
U16 = mybir.dt.uint16
U8 = mybir.dt.uint8
FP8X4 = mybir.dt.float8_e4m3fn_x4
ALU = mybir.AluOpType
COPY = mybir.ActivationFunctionType.Copy

P = 128
PACK = 4
BANK = 512
LANE = 16
HV = V // 2


def tile_picked_laypgappagem_none_p_kernel(
    tc, x_words, x_scales, w1, gn, w2, mem, offs, n1, n2, n3, out
):
    nc = tc.nc
    with ExitStack() as ctx:
        lists = ctx.enter_context(tc.tile_pool(name="lists", bufs=1))
        keep = ctx.enter_context(tc.tile_pool(name="keep", bufs=1))
        psum = ctx.enter_context(tc.psum_pool(name="psum", bufs=1))

        offs_sb = lists.tile([P, S // LANE], U16, name="offs_sb")
        n1_sb = lists.tile([P, S // LANE], U16, name="n1_sb")
        n2_sb = lists.tile([P, V // LANE], U16, name="n2_sb")
        n3_sb = lists.tile([P, U // LANE], U16, name="n3_sb")

        def entries(list_sb, first, count):
            return list_sb[:, first // LANE : (first + count) // LANE]

        scale_table = keep.tile([P, T], U8, name="scale_table", align_bytes=64)
        nc.gpsimd.memset(scale_table[:].bitcast(I32), 0)
        scale_rows = keep.tile([P, T], U8, name="scale_rows", align_bytes=64)
        nc.sync.dma_start(offs_sb[:], offs)
        for q in range(4):
            nc.sync.dma_start(
                out=scale_rows[32 * q : 32 * q + 4, :].bitcast(I32),
                in_=x_scales[0, 4 * q : 4 * q + 4, :].bitcast(I32),
            )
        gain = keep.tile([P, PACK], F32, name="gain")
        nc.sync.dma_start(out=gain[:], in_=gn.rearrange("(p t) o -> p (t o)", t=PACK))
        w1_rows = w1.rearrange("(p j) c -> p j c", j=PACK)
        w1_raw = []
        for half in range(2):
            raw = keep.tile([P, PACK, H // 2], F32, name=f"w1_raw{half}")
            nc.sync.dma_start(out=raw[:], in_=w1_rows[:, :, half * (H // 2) : (half + 1) * (H // 2)])
            w1_raw.append(raw)
        word_table = keep.tile([P, T], U32, name="word_table", align_bytes=64)
        nc.sync.dma_start(
            out=word_table[:].bitcast(I32),
            in_=x_words[0].rearrange("p n r -> p (n r)").bitcast(I32),
        )
        nc.sync.dma_start(n1_sb[:], n1)
        w2_rows = w2.rearrange("(p j) c -> p j c", j=PACK)
        w2_raw = []
        for half in range(2):
            raw = keep.tile([P, PACK, N // 2], F32, name=f"w2_raw{half}")
            nc.sync.dma_start(out=raw[:], in_=w2_rows[:, :, half * (N // 2) : (half + 1) * (N // 2)])
            w2_raw.append(raw)
        nc.sync.dma_start(n2_sb[:], n2)
        mem_rows = mem.rearrange("(p t) w -> t p w", t=PACK)
        out_rows = out.rearrange("(p t) w -> t p w", t=PACK)
        page = []
        for t in range(PACK):
            pg = keep.tile([P, U], F32, name=f"page{t}")
            nc.sync.dma_start(out=pg[:], in_=mem_rows[t])
            page.append(pg)
        nc.sync.dma_start(n3_sb[:], n3)

        def dealt(grouped):
            return grouped[:].rearrange("p (t m j) -> p m j t", t=PACK, j=PACK)

        def quantise(name, values, width):
            codes = keep.tile([P, width], U32, name=name + "_codes", align_bytes=64)
            scales = keep.tile([P, width], U8, name=name + "_scales", align_bytes=64)
            nc.vector.quantize_mx(out=codes[:].bitcast(FP8X4), scales=scales[:], in_=values)
            return codes, scales

        half_gain = keep.tile([P, PACK], F32, name="half_gain")
        positive = keep.tile([P, PACK], F32, name="positive")
        slope = keep.tile([P, PACK], F32, name="slope")
        factor = keep.tile([P, PACK], F32, name="factor")
        nc.gpsimd.tensor_scalar(half_gain[:], gain[:], 0.5, 0.0, ALU.mult, ALU.add)
        nc.gpsimd.tensor_scalar(positive[:], gain[:], 0.0, 1.0, ALU.is_ge, ALU.mult)
        nc.gpsimd.tensor_scalar(slope[:], positive[:], 1.5, -2.0, ALU.mult, ALU.add)
        nc.gpsimd.tensor_scalar(factor[:], positive[:], 3.0, -1.0, ALU.mult, ALU.add)

        for q in range(4):
            rows = slice(32 * q, 32 * q + 4)
            nc.vector.tensor_copy(scale_table[rows, :].bitcast(I32), scale_rows[rows, :].bitcast(I32))
        x_scale = keep.tile([P, S], U8, name="x_scale", align_bytes=64)
        nc.vector.tensor_copy(x_scale[:], scale_table[:].indirect(offs_sb[:]))


        w1_bf = keep.tile([P, PACK * H], BF16, name="w1_bf", align_bytes=64)
        for half in range(2):
            nc.scalar.copy(
                out=dealt(w1_bf)[:, half * 64 : (half + 1) * 64],
                in_=w1_raw[half][:].rearrange("p j (m t) -> p m j t", t=PACK),
            )
        w1_codes, w1_scales = quantise("w1", w1_bf[:], H)


        x_code = []
        for half in range(2):
            xc = keep.tile([P, BANK], U32, name=f"x_code{half}", align_bytes=64)
            nc.vector.tensor_copy(xc[:], word_table[:].indirect(entries(offs_sb, half * BANK, BANK)))
            x_code.append(xc)

        y_bank = {}
        for t, half in ((0, 0), (1, 0), (0, 1), (1, 1), (2, 0), (2, 1), (3, 0), (3, 1)):
            if True:
                bank = psum.tile([P, BANK], F32, name=f"y{t}_{half}", tag=f"bank{PACK * half + t}")
                cols = slice(P * t, P * (t + 1))
                nc.tensor.matmul_mx(
                    out=bank[:],
                    lhsT=w1_codes[:, cols].bitcast(FP8X4),
                    lhsT_scale=w1_scales[:, cols],
                    rhs=x_code[half][:].bitcast(FP8X4),
                    rhs_scale=x_scale[:, half * BANK : (half + 1) * BANK],
                    start=True,
                    stop=True,
                )
                y_bank[t, half] = bank


        y = [keep.tile([P, S], F32, name=f"y_sb{t}") for t in range(PACK)]

        def leave_y(t, half, on_vector):
            dst = y[t][:, half * BANK : (half + 1) * BANK]
            if on_vector:
                nc.vector.tensor_scalar_mul(dst, y_bank[t, half][:], half_gain[:, t : t + 1])
            else:
                nc.scalar.activation(dst, y_bank[t, half][:], COPY, scale=half_gain[:, t : t + 1])

        lined = {}

        def line_up(t, half):
            ln = keep.tile([P, 2 * HV], F32, name=f"lined{t}_{half}", tag=f"lined{t}")
            nc.scalar.activation(ln[:], y[t][:].indirect(entries(n1_sb, half * 2 * HV, 2 * HV)), COPY)
            lined[t, half] = ln

        z_planes = [keep.tile([P, PACK, HV], BF16, name=f"z_planes{half}", tag=f"z_planes{half}") for half in range(2)]

        def make_z(ts, half):
            diff = {t: keep.tile([P, HV], F32, name=f"diff{t}_{half}", tag="z_planes0" if (t, half) == (1, 1) else f"diff{t}_{half}") for t in ts}
            bent = {t: keep.tile([P, HV], F32, name=f"bent{t}_{half}") for t in ts}
            for t in ts:
                ln = lined[t, half]
                nc.vector.tensor_tensor(diff[t][:], ln[:, 1::2], ln[:, 0::2], ALU.subtract)
            for t in ts:
                nc.vector.scalar_tensor_tensor(
                    bent[t][:], diff[t][:], slope[:, t : t + 1], diff[t][:], ALU.mult, ALU.max
                )
            for t in ts:
                nc.vector.scalar_tensor_tensor(
                    z_planes[half][:, t, :], bent[t][:], factor[:, t : t + 1], lined[t, half][:, 0::2], ALU.mult, ALU.add
                )

        z_bf = [keep.tile([P, HV, PACK], BF16, name=f"z_bf{half}", align_bytes=64) for half in range(2)]
        h_bank = {}

        def second_product(half):
            z_codes, z_scales = quantise(f"z{half}", z_bf[half][:].rearrange("p v t -> p (v t)"), HV)
            for t in range(PACK):
                bank = psum.tile([P, HV], F32, name=f"h{t}_{half}", tag=f"bank{PACK * half + t}")
                cols = slice(P * t, P * (t + 1))
                nc.tensor.matmul_mx(
                    out=bank[:],
                    lhsT=w2_codes[:, cols].bitcast(FP8X4),
                    lhsT_scale=w2_scales[:, cols],
                    rhs=z_codes[:].bitcast(FP8X4),
                    rhs_scale=z_scales[:],
                    start=True,
                    stop=True,
                )
                h_bank[t, half] = bank

        def leave_h(dst, t, half):
            nc.scalar.copy(out=dst, in_=h_bank[t, half][:])

        def put(t, first, count, values):
            nc.vector.tensor_copy(page[t][:].indirect(entries(n2_sb, first, count)), values)

        def finish(t, first, count, fetch_on_vector, add_engine):
            cols = slice(first, first + count)
            fetched = keep.tile([P, count], F32, name=f"fetched{t}_{first}")
            result = keep.tile([P, count], F32, name=f"result{t}_{first}")
            window = page[t][:].indirect(entries(n3_sb, first, count))
            if fetch_on_vector:
                nc.vector.tensor_scalar(fetched[:], window, -0.5, 0.0, ALU.mult, ALU.add)
            else:
                nc.scalar.activation(fetched[:], window, COPY, scale=-0.5)
            add_engine.tensor_tensor(result[:], fetched[:], page[t][:, cols], ALU.add)
            nc.sync.dma_start(out=out_rows[t][:, cols], in_=result[:])

        w2_bf = keep.tile([P, PACK * N], BF16, name="w2_bf", align_bytes=64)
        nc.scalar.copy(out=dealt(w2_bf)[:, 0:64], in_=w2_raw[0][:].rearrange("p j (m t) -> p m j t", t=PACK))
        for t, half in ((0, 0), (1, 0), (0, 1), (1, 1), (2, 0), (2, 1), (3, 0), (3, 1)):
            leave_y(t, half, t >= 2 or (t, half) == (0, 1))
        nc.vector.tensor_copy(out=dealt(w2_bf)[:, 64:128], in_=w2_raw[1][:].rearrange("p j (m t) -> p m j t", t=PACK))
        w2_codes, w2_scales = quantise("w2", w2_bf[:], N)
        for t in range(PACK):
            line_up(t, 0)
        make_z((0, 1), 0)
        make_z((2, 3), 0)
        line_up(0, 1)
        line_up(1, 1)
        nc.vector.tensor_copy(out=z_bf[0][:], in_=z_planes[0][:].rearrange("p t v -> p v t"))
        second_product(0)
        line_up(2, 1)
        line_up(3, 1)
        make_z((0, 1), 1)
        make_z((2, 3), 1)
        h = {t: keep.tile([P, V], F32, name=f"h{t}") for t in (2, 3)}
        for t in (2, 3):
            leave_h(h[t][:, :HV], t, 0)
        h0_low = keep.tile([P, HV], F32, name="h0_low", tag="diff3_1")
        h0_high = keep.tile([P, HV], F32, name="h0_high")
        leave_h(h0_low[:], 0, 0)
        nc.scalar.copy(out=z_bf[1][:], in_=z_planes[1][:].rearrange("p t v -> p v t"))
        h1_low = keep.tile([P, HV], F32, name="h1_low", tag="z_planes1")
        h1_high = keep.tile([P, HV], F32, name="h1_high")
        leave_h(h1_low[:], 1, 0)
        second_product(1)
        leave_h(h0_high[:], 0, 1)
        leave_h(h1_high[:], 1, 1)
        leave_h(h[2][:, HV:], 2, 1)
        leave_h(h[3][:, HV:], 3, 1)
        put(0, 0, HV, h0_low[:])
        put(0, HV, HV, h0_high[:])
        put(1, 0, HV, h1_low[:])
        put(1, HV, HV, h1_high[:])
        for t in range(PACK - 1):
            finish(t, 0, BANK, False, nc.gpsimd)
            finish(t, BANK, BANK, False, nc.gpsimd)
            if t < 2:
                put(t + 2, 0, V, h[t + 2][:])
        finish(3, 0, 320, False, nc.vector)
        finish(3, 640, 384, True, nc.vector)
        finish(3, 320, 320, False, nc.vector)
